import numpy as np
import ml_dtypes


def mxq(x, axis, fmt="e4m3"):
    dtype, down = {"e4m3": (ml_dtypes.float8_e4m3fn, 7), "e5m2": (ml_dtypes.float8_e5m2, 14)}[fmt]
    v = np.moveaxis(np.asarray(x, np.float32).astype(ml_dtypes.bfloat16).astype(np.float64), axis, -1)
    blocks = v.reshape(v.shape[:-1] + (-1, 32))
    amax = np.abs(blocks).max(-1, keepdims=True)
    byte = np.maximum(np.where(amax > 0, np.frexp(amax)[1] - 1 + 127, 0) - down, 1)
    scale = np.exp2(byte - 127.0)
    codes = (blocks / scale).astype(np.float32).astype(dtype).astype(np.float64)
    return np.moveaxis((codes * scale).reshape(v.shape), -1, axis)


WIDE = False


def mx_kscale(k):
    if not WIDE:
        return np.ones(k)
    levels = np.array([10, -10, 5, -5, 0])
    if k % 512:
        return np.exp2(np.random.permutation(np.resize(levels, k // 32))).repeat(32)
    a = np.empty((k // 512, 16))
    for p in range(k // 512):
        a[p, :8] = np.random.permutation(np.resize(levels, 8))
        for g in range(8):
            far = levels[np.abs(levels - a[p, g]) >= 10]
            a[p, g + 8] = far[np.random.randint(len(far))]
    return np.exp2(a.ravel()).repeat(32)


def f64(x):
    return np.asarray(x).astype(np.float64)


def striped(idx):
    return np.tile(idx.reshape(-1, 16).T, (8, 1)).astype(np.uint16)


def unstriped(offs):
    return offs[:16].T.reshape(-1).astype(np.int64)


E2M1 = np.array([0.0, 0.5, 1.0, 1.5, 2.0, 3.0, 4.0, 6.0, -0.0, -0.5, -1.0, -1.5, -2.0, -3.0, -4.0, -6.0])


def pack_weight(w, fmt):
    k, n = w.shape
    w = f64(np.asarray(w, np.float32).astype(ml_dtypes.bfloat16)).reshape(k // 32, 32, n)
    amax = np.abs(w).max(1)
    if fmt == "e4m3":
        byte = np.frexp(amax)[1] - 1 + 127 - 7
    else:
        mant, ex = np.frexp(amax / 6.0)
        byte = np.where(mant > 0.5, ex, ex - 1) + 127
    byte = np.clip(np.where(amax > 0, byte, 1), 1, 254)
    scaled = (w * np.exp2(127.0 - byte)[:, None, :]).reshape(k, n).astype(np.float32)
    by_word = np.ascontiguousarray(scaled.reshape(k // 512, 128, 4, n).transpose(0, 1, 3, 2))
    if fmt == "e4m3":
        words = by_word.astype(ml_dtypes.float8_e4m3fn).view(np.uint8)
    else:
        c = by_word.astype(ml_dtypes.float4_e2m1fn).view(np.uint8) & 0xF
        words = (c[..., 0::2] | (c[..., 1::2] << 4)).reshape(k // 512, 128, 2 * n)
    return np.ascontiguousarray(words), np.ascontiguousarray(byte.astype(np.uint8).reshape(k // 512, 16, n))


def unpack_weight(words, scales, fmt):
    g, _, n = scales.shape
    words = np.ascontiguousarray(words).reshape(g, 128, n, -1)
    if fmt == "e4m3":
        vals = words.view(ml_dtypes.float8_e4m3fn).astype(np.float64)
    else:
        nib = np.empty((g, 128, n, 4), np.uint8)
        nib[..., 0::2] = words & 0xF
        nib[..., 1::2] = words >> 4
        vals = E2M1[nib]
    vals = vals * np.repeat(np.exp2(scales.astype(np.float64) - 127.0), 8, axis=1)[..., None]
    return vals.transpose(0, 1, 3, 2).reshape(g * 512, n)


def gelu(v):
    return 0.5 * v * (1.0 + np.tanh(np.sqrt(2.0 / np.pi) * (v + 0.044715 * v**3)))


K, H, T, S, T2, P = 1024, 512, 4096, 1024, 2048, 1024

def setup_inputs():
    n = np.random.standard_normal
    s, u = mx_kscale(K)[:, None], mx_kscale(H)[:, None]
    tab_words, tab_scales = pack_weight(n((K, T)) * s, "e4m3")
    w2_words, w2_scales = pack_weight(n((K, H)) / np.sqrt(K) / s * u.T, "e2m1")
    w4_words, w4_scales = pack_weight(n((H, H)) / np.sqrt(H) / u * u.T, "e4m3")
    return {
        "tab_words": tab_words, "tab_scales": tab_scales,
        "offs": striped(np.random.permutation(T)[:S]),
        "w1": (n((K, H)) / np.sqrt(K) / s * u.T).astype(np.float32),
        "w2_words": w2_words, "w2_scales": w2_scales,
        "w3": (n((K, H)) / np.sqrt(K) / s * u.T).astype(np.float32),
        "page0": (n((H, T2)) * u).astype(np.float32),
        "wgs": np.exp(0.3 * n((128, S))).astype(np.float32),
        "offs2": striped(np.random.permutation(T2)[:S]),
        "offs3": striped(np.random.permutation(T2)[:P]),
        "gain": (np.random.choice([-1.0, 1.0], H) * np.exp(0.3 * n(H))).astype(np.float32),
        "w4_words": w4_words, "w4_scales": w4_scales,
        "wgo": np.exp(0.3 * n((128, P))).astype(np.float32),
        "offs4": striped(np.random.permutation(T2)[:P]),
    }

def reference(tab_words, tab_scales, offs, w1, w2_words, w2_scales, w3, page0, wgs, offs2, offs3, gain,
              w4_words, w4_scales, wgo, offs4):
    v = unpack_weight(tab_words, tab_scales, "e4m3")[:, unstriped(offs)]
    w2 = unpack_weight(w2_words, w2_scales, "e2m1")
    w4 = unpack_weight(w4_words, w4_scales, "e4m3")
    low = np.minimum(mxq(f64(w1), 0, "e4m3").T @ v, w2.T @ v)
    h = low + (mxq(f64(w3), 0, "e4m3").T @ v)
    page = f64(page0).copy()
    page[:, unstriped(offs2)] = np.tile(f64(wgs), (H // 128, 1)) * h
    x = np.abs(page[:, unstriped(offs3)]) * f64(gain)[:, None]
    y = (w4.T @ mxq(x, 0, "e4m3")) + x
    page[:, unstriped(offs4)] = np.tile(f64(wgo), (H // 128, 1)) * y
    return page

@@ -1,0 +1,316 @@
+from contextlib import ExitStack
+
+import concourse.mybir as mybir
+from concourse.masks import make_identity
+
+K, H, T, S, T2 = 1024, 512, 4096, 1024, 2048
+FLOPS = 2 * (3 * K * H * S + H * H * S)
+
+F32 = mybir.dt.float32
+BF16 = mybir.dt.bfloat16
+I32 = mybir.dt.int32
+U32 = mybir.dt.uint32
+U16 = mybir.dt.uint16
+U8 = mybir.dt.uint8
+FP8X4 = mybir.dt.float8_e4m3fn_x4
+FP4X4 = mybir.dt.float4_e2m1fn_x4
+ALU = mybir.AluOpType
+ACT = mybir.ActivationFunctionType
+
+P = 128
+PACK = 4
+PASSES = K // (P * PACK)
+TILES = H // P
+HALF = 512
+HALVES = S // HALF
+BLOCKS = HALF // P
+LIST_COLS = HALF // 16
+
+
+def tile_list_short_shot_slots_kernel(
+    tc, tab_words, tab_scales, offs, w1, w2_words, w2_scales, w3, page0, wgs, offs2, offs3, gain,
+    w4_words, w4_scales, wgo, offs4, out,
+):
+    nc = tc.nc
+    with ExitStack() as ctx:
+        lists = ctx.enter_context(tc.tile_pool(name="lists", bufs=1))
+        keep = ctx.enter_context(tc.tile_pool(name="keep", bufs=1))
+        psum = ctx.enter_context(tc.psum_pool(name="psum", bufs=1))
+
+        def half_of(list_tile, h):
+            return list_tile[:, h * LIST_COLS : (h + 1) * LIST_COLS]
+
+        def load_list(source, name):
+            tile = lists.tile([P, S // 16], U16, name=name)
+            nc.sync.dma_start(tile[:], source)
+            return tile
+
+        def load_scale_rows(queue, tile, source):
+            for q in range(4):
+                queue.dma_start(
+                    tile[32 * q : 32 * q + 4].bitcast(I32),
+                    source[:, 4 * q : 4 * q + 4, :].rearrange("a r n -> r a n").bitcast(I32),
+                )
+
+        def load_weight(source, t):
+            raw = keep.tile([P, PACK, PASSES, P], F32, name="w_raw", bufs=4)
+            for a in range(PASSES):
+                rows = source[512 * a : 512 * (a + 1), P * t : P * (t + 1)]
+                nc.sync.dma_start(raw[:, :, a, :], rows.rearrange("(p j) c -> p j c", j=PACK))
+            return raw
+
+        def load_page(t):
+            page = keep.tile([P, T2], F32, name="page%d" % t)
+            nc.sync.dma_start(page[:], page0[P * t : P * (t + 1), :])
+            return page
+
+        def load_half(source, h, name):
+            tile = keep.tile([P, HALF], F32, name=name)
+            nc.sync.dma_start(tile[:], source[:, h * HALF : (h + 1) * HALF])
+            return tile
+
+        def load_table(a):
+            tile = keep.tile([P, T], U32, name="table%d" % a)
+            nc.sync.dma_start(tile[:].bitcast(I32), tab_words[a].rearrange("p n i -> p (n i)").bitcast(I32))
+            return tile
+
+        table_scales = keep.tile([P, PASSES, T], U8, name="table_scales")
+        nc.vector.memset(table_scales[:].bitcast(I32), 0)
+
+        w2_planes = keep.tile([P, PASSES, H], U8, name="w2_planes", align_bytes=64)
+        w4_plane = keep.tile([P, 1, H], U8, name="w4_plane", align_bytes=64)
+        nc.gpsimd.memset(w2_planes[:].bitcast(I32), 0)
+        load_scale_rows(nc.gpsimd, w2_planes, w2_scales)
+        ident = keep.tile([P, P], F32, name="ident")
+        make_identity(nc, ident[:])
+        ident_bf = keep.tile([P, P], BF16, name="ident_bf")
+        make_identity(nc, ident_bf[:])
+        nc.gpsimd.memset(w4_plane[:].bitcast(I32), 0)
+        load_scale_rows(nc.gpsimd, w4_plane, w4_scales)
+
+        raw1, raw3, pages = {}, {}, {}
+        idx = load_list(offs, "idx")
+        idx2 = load_list(offs2, "idx2")
+        idx3 = load_list(offs3, "idx3")
+        idx4 = load_list(offs4, "idx4")
+        raw1[0] = load_weight(w1, 0)
+        w2_codes = keep.tile([P, PASSES, 2 * H], U8, name="w2_codes", align_bytes=64)
+        nc.sync.dma_start(w2_codes[:].bitcast(I32), w2_words.rearrange("a p n -> p a n").bitcast(I32))
+        wgs_half = [load_half(wgs, 0, "wgs0")]
+        load_scale_rows(nc.sync, table_scales, tab_scales)
+        table = [load_table(0), load_table(1)]
+        raw3[0] = load_weight(w3, 0)
+        pages[0] = load_page(0)
+        raw1[1] = load_weight(w1, 1)
+        wgs_half.append(load_half(wgs, 1, "wgs1"))
+        raw3[1] = load_weight(w3, 1)
+        gains = keep.tile([P, TILES], F32, name="gains")
+        with nc.allow_non_contiguous_dma(reason="one gain for each row of a page tile"):
+            nc.sync.dma_start(gains[:], gain.rearrange("(t p) -> p t", p=P))
+
+        codes1, codes3 = {}, {}
+
+        def quantize_weight(raw, name):
+            grouped = keep.tile([P, PASSES, P, PACK], BF16, name="w_grouped", bufs=3, align_bytes=64)
+            nc.scalar.activation(
+                grouped[:].rearrange("p a (c i) j -> p (a c) j i", i=4),
+                raw[:].rearrange("p j a (c i) -> p (a c) j i", i=4),
+                ACT.Copy,
+            )
+            codes = keep.tile([P, PASSES * P], U32, name=name + "_codes", align_bytes=64)
+            plane = keep.tile([P, PASSES * P], U8, name=name + "_plane", align_bytes=64)
+            nc.vector.quantize_mx(codes[:].bitcast(FP8X4), plane[:], grouped[:].rearrange("p a c j -> p (a c j)"))
+            return codes, plane
+
+        def quantize_weights(t):
+            codes1[t] = quantize_weight(raw1[t], "w1_%d" % t)
+            codes3[t] = quantize_weight(raw3[t], "w3_%d" % t)
+
+        picked_words, picked_scales = {}, {}
+        for h in range(HALVES):
+            for a in range(PASSES):
+                plane = keep.tile([P, HALF], U8, name="picked_scales%d%d" % (a, h), align_bytes=64)
+                nc.vector.tensor_copy(plane[:], table_scales[:, a, :].indirect(half_of(idx, h)))
+                picked_scales[a, h] = plane
+            if h == 0:
+                quantize_weights(0)
+            for a in range(PASSES):
+                words = keep.tile([P, HALF], U32, name="picked_words%d%d" % (a, h), align_bytes=64)
+                nc.vector.tensor_copy(words[:], table[a][:].indirect(half_of(idx, h)))
+                picked_words[a, h] = words
+
+        def weight_operands(t):
+            cols = slice(P * t, P * (t + 1))
+            by_pass = [slice(P * a, P * (a + 1)) for a in range(PASSES)]
+            return (
+                [(codes1[t][0][:, c].bitcast(FP8X4), codes1[t][1][:, c]) for c in by_pass],
+                [(w2_codes[:, a, 2 * P * t : 2 * P * (t + 1)].bitcast(FP4X4), w2_planes[:, a, cols]) for a in range(PASSES)],
+                [(codes3[t][0][:, c].bitcast(FP8X4), codes3[t][1][:, c]) for c in by_pass],
+            )
+
+        def product_banks():
+            first = psum.tile([P, HALF], F32, name="first")
+            second = psum.tile([P, HALF], F32, name="second", bufs=2)
+            third = psum.tile([P, HALF], F32, name="third")
+            return first, second, third
+
+        def smaller_of(first, second):
+            first_sb = keep.tile([P, HALF], F32, name="first_sb", bufs=2)
+            nc.scalar.copy(first_sb[:], first[:])
+            low = keep.tile([P, HALF], F32, name="low", bufs=2)
+            nc.vector.tensor_tensor(low[:], second[:], first_sb[:], ALU.min)
+            return low
+
+        def opening_stage():
+            banks = product_banks()
+            for bank, operands in zip(banks, weight_operands(0)):
+                for a, (codes, plane) in enumerate(operands):
+                    nc.tensor.matmul_mx(
+                        bank[:], lhsT=codes, lhsT_scale=plane,
+                        rhs=picked_words[a, 0][:].bitcast(FP8X4), rhs_scale=picked_scales[a, 0][:],
+                        start=(a == 0), stop=(a == PASSES - 1),
+                    )
+            low = smaller_of(banks[0], banks[1])
+            hidden = keep.tile([P, HALF], F32, name="hidden", bufs=3)
+            nc.vector.tensor_tensor(hidden[:], banks[2][:], low[:], ALU.add)
+            return hidden
+
+        def first_stage(t, h):
+            banks = product_banks()
+            for bank, operands in zip(banks, weight_operands(t)):
+                for a, (codes, plane) in enumerate(operands):
+                    for b in range(BLOCKS):
+                        entries = slice(P * b, P * (b + 1))
+                        nc.tensor.matmul_mx(
+                            bank[:, entries],
+                            lhsT=picked_words[a, h][:, entries].bitcast(FP8X4),
+                            lhsT_scale=picked_scales[a, h][:, entries],
+                            rhs=codes,
+                            rhs_scale=plane,
+                            start=(a == 0 and b == 0),
+                            stop=(a == PASSES - 1 and b == BLOCKS - 1),
+                        )
+            low = smaller_of(banks[0], banks[1])
+            tag = "sizes%d" % (t - 1) if h == 1 and t > 0 else "third_sb%d" % h
+            third_sb = keep.tile([P, HALF], F32, name="third_sb", tag=tag)
+            nc.scalar.copy(third_sb[:], banks[2][:])
+            return low, third_sb
+
+        def add_and_turn(low, third_sb):
+            summed = psum.tile([P, HALF], F32, name="summed")
+            for b in range(BLOCKS):
+                cols = slice(P * b, P * (b + 1))
+                nc.tensor.matmul(summed[:, cols], third_sb[:, cols], ident[:], start=True, stop=False, is_transpose=True)
+                nc.tensor.matmul(summed[:, cols], low[:, cols], ident[:], start=False, stop=True, is_transpose=True)
+            hidden = keep.tile([P, HALF], F32, name="hidden", bufs=3)
+            nc.scalar.copy(hidden[:], summed[:])
+            return hidden
+
+        def put(t, values, weights, list_tile, h):
+            nc.vector.tensor_tensor(pages[t][:].indirect(half_of(list_tile, h)), values, weights[h][:], ALU.mult)
+
+        def fetch(t, h, dest):
+            nc.vector.tensor_copy(dest, pages[t][:].indirect(half_of(idx3, h)))
+
+        def prepare(t, fetched, size, turned):
+            nc.scalar.activation(size, fetched, ACT.Abs)
+            rounded = keep.tile([P, HALF], BF16, name="rounded", bufs=2)
+            nc.scalar.activation(rounded[:], size, ACT.Copy, scale=gains[:, t : t + 1])
+            bank = psum.tile([P, BLOCKS, P], BF16, name="turn")
+            for b in range(BLOCKS):
+                nc.tensor.transpose(bank[:, b, :], rounded[:, P * b : P * (b + 1)], ident_bf[:])
+            nc.scalar.copy(turned[:, :, P * t : P * (t + 1)], bank[:])
+
+        def quantize_half(turned, grouped, name):
+            pairs = turned[:].bitcast(F32)
+            for b0 in range(0, BLOCKS, 2):
+                bank = psum.tile([P, 2, 2, P], F32, name="pairs", bufs=2)
+                for b in range(2):
+                    for u in range(2):
+                        nc.tensor.transpose(bank[:, b, u, :], pairs[:, b0 + b, u : 2 * P : 2], ident[:])
+                dest = grouped[:, P * PACK * b0 : P * PACK * (b0 + 2)].bitcast(F32)
+                nc.scalar.copy(dest.rearrange("p (b e u) -> p b e u", b=2, u=2), bank[:].rearrange("p b u e -> p b e u"))
+            codes = keep.tile([P, HALF], U32, name=name + "_codes", align_bytes=64)
+            plane = keep.tile([P, HALF], U8, name=name + "_plane", align_bytes=64)
+            nc.vector.quantize_mx(codes[:].bitcast(FP8X4), plane[:], grouped[:])
+            return codes, plane
+
+        sizes = {}
+        turned0 = keep.tile([P, BLOCKS, H], BF16, name="turned0", tag="turned0")
+        units = [(t, h) for t in range(TILES) for h in range(HALVES)]
+        fetched = {}
+
+        def prepare_early(t):
+            size = keep.tile([P, HALF], F32, name="size", tag="sizes%d" % t)
+            sizes[t, 0] = size[:]
+            prepare(t, fetched[t][:], sizes[t, 0], turned0)
+
+        for u, (t, h) in enumerate(units):
+            if h == 0 and t + 2 < TILES:
+                raw1[t + 2] = load_weight(w1, t + 2)
+                raw3[t + 2] = load_weight(w3, t + 2)
+            if h == 0 and t + 1 < TILES:
+                pages[t + 1] = load_page(t + 1)
+            if u == 0:
+                put(t, opening_stage()[:], wgs_half, idx2, h)
+            current = ahead if u > 0 else None
+            if h == 0 and t + 1 < TILES:
+                quantize_weights(t + 1)
+            if u + 1 < len(units):
+                ahead = first_stage(*units[u + 1])
+            if u > 0:
+                put(t, add_and_turn(*current)[:], wgs_half, idx2, h)
+            if h == 1:
+                if t > 0:
+                    prepare_early(t - 1)
+                fetched[t] = keep.tile([P, HALF], F32, name="fetched", bufs=2)
+                fetch(t, 0, fetched[t][:])
+        prepare_early(TILES - 1)
+
+        w4_codes = keep.tile([P, H], U32, name="w4_codes", align_bytes=64)
+        nc.sync.dma_start(w4_codes[:].bitcast(I32), w4_words[0].rearrange("p n i -> p (n i)").bitcast(I32))
+        wgo_half = [load_half(wgo, h, "wgo%d" % h) for h in range(HALVES)]
+
+        late = keep.tile([P, TILES - 1, HALF], F32, name="late", tag="wgs1")
+        for t in range(TILES - 1):
+            fetch(t, 1, late[:, t, :])
+        grouped0 = keep.tile([P, HALF * PACK], BF16, name="grouped0", tag="grouped0", align_bytes=64)
+        x_codes = [quantize_half(turned0, grouped0, "x0")]
+        last = keep.tile([P, HALF], F32, name="last", tag="grouped0", align_bytes=64)
+        fetch(TILES - 1, 1, last[:])
+
+        def second_stage(t, h, result):
+            bank = psum.tile([P, HALF], F32, name="mixed", tag="second", bufs=2)
+            cols = slice(P * t, P * (t + 1))
+            nc.tensor.matmul_mx(
+                bank[:], lhsT=w4_codes[:, cols].bitcast(FP8X4), lhsT_scale=w4_plane[:, 0, cols],
+                rhs=x_codes[h][0][:].bitcast(FP8X4), rhs_scale=x_codes[h][1][:], start=True, stop=True,
+            )
+            nc.vector.scalar_tensor_tensor(result, sizes[t, h], gains[:, t : t + 1], bank[:], ALU.mult, ALU.add)
+
+        sizes1 = keep.tile([P, TILES, HALF], F32, name="sizes1", tag="turned0")
+        turned1 = keep.tile([P, BLOCKS, H], BF16, name="turned1")
+        results = {}
+        for t in range(TILES - 1):
+            results[t] = keep.tile([P, HALF], F32, name="result", bufs=3)
+            second_stage(t, 0, results[t][:])
+            if t > 0:
+                put(t - 1, results[t - 1][:], wgo_half, idx4, 0)
+        for t in range(TILES):
+            sizes[t, 1] = sizes1[:, t, :]
+            prepare(t, late[:, t, :] if t < TILES - 1 else last[:], sizes[t, 1], turned1)
+        grouped1 = keep.tile([P, HALF * PACK], BF16, name="grouped1", tag="grouped1", align_bytes=64)
+        x_codes.append(quantize_half(turned1, grouped1, "x1"))
+        put(TILES - 2, results[TILES - 2][:], wgo_half, idx4, 0)
+        held = keep.tile([P, HALF], F32, name="held", tag="grouped1", align_bytes=64)
+        second_stage(TILES - 1, 0, held[:])
+        previous = (TILES - 1, held, 0)
+        for t in range(TILES):
+            result = keep.tile([P, HALF], F32, name="result", bufs=3)
+            second_stage(t, 1, result[:])
+            put(previous[0], previous[1][:], wgo_half, idx4, previous[2])
+            if previous[2] == 1:
+                nc.sync.dma_start(out[P * previous[0] : P * (previous[0] + 1), :], pages[previous[0]][:])
+            previous = (t, result, 1)
+        put(previous[0], previous[1][:], wgo_half, idx4, 1)
+        nc.sync.dma_start(out[P * previous[0] : P * (previous[0] + 1), :], pages[previous[0]][:])

@@ -45,9 +45,9 @@ def tile_list_short_shot_slots_kernel(
             nc.sync.dma_start(tile[:], source)
             return tile
 
-        def load_scale_rows(queue, tile, source):
+        def load_scale_rows(tile, source):
             for q in range(4):
-                queue.dma_start(
+                nc.sync.dma_start(
                     tile[32 * q : 32 * q + 4].bitcast(I32),
                     source[:, 4 * q : 4 * q + 4, :].rearrange("a r n -> r a n").bitcast(I32),
                 )
@@ -58,6 +58,12 @@ def tile_list_short_shot_slots_kernel(
                 rows = source[512 * a : 512 * (a + 1), P * t : P * (t + 1)]
                 nc.sync.dma_start(raw[:, :, a, :], rows.rearrange("(p j) c -> p j c", j=PACK))
             return raw
+
+        def load_w2(first, count):
+            tile = keep.tile([P, PASSES, 2 * P * count], U8, name="w2_codes%d" % first, align_bytes=64)
+            words = w2_words[:, :, 2 * P * first : 2 * P * (first + count)]
+            nc.sync.dma_start(tile[:].bitcast(I32), words.rearrange("a p n -> p a n").bitcast(I32))
+            return [tile[:, :, 2 * P * i : 2 * P * (i + 1)] for i in range(count)]
 
         def load_page(t):
             page = keep.tile([P, T2], F32, name="page%d" % t)
@@ -80,33 +86,30 @@ def tile_list_short_shot_slots_kernel(
         w2_planes = keep.tile([P, PASSES, H], U8, name="w2_planes", align_bytes=64)
         w4_plane = keep.tile([P, 1, H], U8, name="w4_plane", align_bytes=64)
         nc.gpsimd.memset(w2_planes[:].bitcast(I32), 0)
-        load_scale_rows(nc.gpsimd, w2_planes, w2_scales)
         ident = keep.tile([P, P], F32, name="ident")
         make_identity(nc, ident[:])
-        ident_bf = keep.tile([P, P], BF16, name="ident_bf")
-        make_identity(nc, ident_bf[:])
         nc.gpsimd.memset(w4_plane[:].bitcast(I32), 0)
-        load_scale_rows(nc.gpsimd, w4_plane, w4_scales)
 
         raw1, raw3, pages = {}, {}, {}
         idx = load_list(offs, "idx")
         idx2 = load_list(offs2, "idx2")
         idx3 = load_list(offs3, "idx3")
         idx4 = load_list(offs4, "idx4")
+        w2_codes = load_w2(0, 1)
         raw1[0] = load_weight(w1, 0)
-        w2_codes = keep.tile([P, PASSES, 2 * H], U8, name="w2_codes", align_bytes=64)
-        nc.sync.dma_start(w2_codes[:].bitcast(I32), w2_words.rearrange("a p n -> p a n").bitcast(I32))
-        wgs_half = [load_half(wgs, 0, "wgs0")]
-        load_scale_rows(nc.sync, table_scales, tab_scales)
-        table = [load_table(0), load_table(1)]
         raw3[0] = load_weight(w3, 0)
+        load_scale_rows(table_scales, tab_scales)
+        table = [load_table(0), load_table(1)]
+        load_scale_rows(w2_planes, w2_scales)
         pages[0] = load_page(0)
+        wgs_half = [load_half(wgs, 0, "wgs0")]
         raw1[1] = load_weight(w1, 1)
-        wgs_half.append(load_half(wgs, 1, "wgs1"))
+        w2_codes.extend(load_w2(1, TILES - 1))
         raw3[1] = load_weight(w3, 1)
         gains = keep.tile([P, TILES], F32, name="gains")
         with nc.allow_non_contiguous_dma(reason="one gain for each row of a page tile"):
             nc.sync.dma_start(gains[:], gain.rearrange("(t p) -> p t", p=P))
+        wgs_half.append(load_half(wgs, 1, "wgs1"))
 
         codes1, codes3 = {}, {}
 
@@ -144,7 +147,7 @@ def tile_list_short_shot_slots_kernel(
             by_pass = [slice(P * a, P * (a + 1)) for a in range(PASSES)]
             return (
                 [(codes1[t][0][:, c].bitcast(FP8X4), codes1[t][1][:, c]) for c in by_pass],
-                [(w2_codes[:, a, 2 * P * t : 2 * P * (t + 1)].bitcast(FP4X4), w2_planes[:, a, cols]) for a in range(PASSES)],
+                [(w2_codes[t][:, a, :].bitcast(FP4X4), w2_planes[:, a, cols]) for a in range(PASSES)],
                 [(codes3[t][0][:, c].bitcast(FP8X4), codes3[t][1][:, c]) for c in by_pass],
             )
 
@@ -161,13 +164,13 @@ def tile_list_short_shot_slots_kernel(
             nc.vector.tensor_tensor(low[:], second[:], first_sb[:], ALU.min)
             return low
 
-        def opening_stage():
+        def opening_stage(h):
             banks = product_banks()
             for bank, operands in zip(banks, weight_operands(0)):
                 for a, (codes, plane) in enumerate(operands):
                     nc.tensor.matmul_mx(
                         bank[:], lhsT=codes, lhsT_scale=plane,
-                        rhs=picked_words[a, 0][:].bitcast(FP8X4), rhs_scale=picked_scales[a, 0][:],
+                        rhs=picked_words[a, h][:].bitcast(FP8X4), rhs_scale=picked_scales[a, h][:],
                         start=(a == 0), stop=(a == PASSES - 1),
                     )
             low = smaller_of(banks[0], banks[1])
@@ -209,108 +212,136 @@ def tile_list_short_shot_slots_kernel(
         def put(t, values, weights, list_tile, h):
             nc.vector.tensor_tensor(pages[t][:].indirect(half_of(list_tile, h)), values, weights[h][:], ALU.mult)
 
-        def fetch(t, h, dest):
-            nc.vector.tensor_copy(dest, pages[t][:].indirect(half_of(idx3, h)))
+        def fetch(t, first, dest):
+            count = dest.shape[1]
+            entries = idx3[:, first // 16 : (first + count) // 16]
+            nc.vector.tensor_copy(dest, pages[t][:].indirect(entries))
 
-        def prepare(t, fetched, size, turned):
+        def prepare(t, fetched, x, turned, size=None):
+            count = fetched.shape[1]
+            if size is None:
+                size = keep.tile([P, count], F32, name="size", bufs=2)[:]
             nc.scalar.activation(size, fetched, ACT.Abs)
-            rounded = keep.tile([P, HALF], BF16, name="rounded", bufs=2)
-            nc.scalar.activation(rounded[:], size, ACT.Copy, scale=gains[:, t : t + 1])
-            bank = psum.tile([P, BLOCKS, P], BF16, name="turn")
-            for b in range(BLOCKS):
-                nc.tensor.transpose(bank[:, b, :], rounded[:, P * b : P * (b + 1)], ident_bf[:])
-            nc.scalar.copy(turned[:, :, P * t : P * (t + 1)], bank[:])
+            nc.scalar.activation(x, size, ACT.Copy, scale=gains[:, t : t + 1])
+            bank = psum.tile([P, count // P, P], F32, name="turn", tag="pairs", bufs=3)
+            for b in range(count // P):
+                nc.tensor.transpose(bank[:, b, :], x[:, P * b : P * (b + 1)], ident[:])
+            nc.scalar.copy(
+                turned.rearrange("p b (u t q e) -> p t b u q e", u=2, t=TILES, e=2)[:, t],
+                bank[:].rearrange("p b (q u e) -> p b u q e", u=2, e=2),
+            )
 
         def quantize_half(turned, grouped, name):
-            pairs = turned[:].bitcast(F32)
-            for b0 in range(0, BLOCKS, 2):
-                bank = psum.tile([P, 2, 2, P], F32, name="pairs", bufs=2)
+            for i, quarter in enumerate(turned):
+                pairs = quarter[:].bitcast(F32)
+                bank = psum.tile([P, 2, 2, P], F32, name="pairs", bufs=3)
                 for b in range(2):
                     for u in range(2):
-                        nc.tensor.transpose(bank[:, b, u, :], pairs[:, b0 + b, u : 2 * P : 2], ident[:])
-                dest = grouped[:, P * PACK * b0 : P * PACK * (b0 + 2)].bitcast(F32)
+                        nc.tensor.transpose(bank[:, b, u, :], pairs[:, b, P * u : P * (u + 1)], ident[:])
+                dest = grouped[:, 2 * P * PACK * i : 2 * P * PACK * (i + 1)].bitcast(F32)
                 nc.scalar.copy(dest.rearrange("p (b e u) -> p b e u", b=2, u=2), bank[:].rearrange("p b u e -> p b e u"))
             codes = keep.tile([P, HALF], U32, name=name + "_codes", align_bytes=64)
             plane = keep.tile([P, HALF], U8, name=name + "_plane", align_bytes=64)
             nc.vector.quantize_mx(codes[:].bitcast(FP8X4), plane[:], grouped[:])
             return codes, plane
 
-        sizes = {}
+        xs = {}
         turned0 = keep.tile([P, BLOCKS, H], BF16, name="turned0", tag="turned0")
         units = [(t, h) for t in range(TILES) for h in range(HALVES)]
         fetched = {}
 
         def prepare_early(t):
             size = keep.tile([P, HALF], F32, name="size", tag="sizes%d" % t)
-            sizes[t, 0] = size[:]
-            prepare(t, fetched[t][:], sizes[t, 0], turned0)
+            xs[t, 0] = keep.tile([P, HALF], F32, name="x%d" % t)
+            prepare(t, fetched[t][:], xs[t, 0][:], turned0[:], size[:])
 
+        products = {}
         for u, (t, h) in enumerate(units):
             if h == 0 and t + 2 < TILES:
                 raw1[t + 2] = load_weight(w1, t + 2)
                 raw3[t + 2] = load_weight(w3, t + 2)
             if h == 0 and t + 1 < TILES:
                 pages[t + 1] = load_page(t + 1)
-            if u == 0:
-                put(t, opening_stage()[:], wgs_half, idx2, h)
-            current = ahead if u > 0 else None
-            if h == 0 and t + 1 < TILES:
+            if t == 0:
+                put(t, opening_stage(h)[:], wgs_half, idx2, h)
+            if (h == 0 and 0 < t < TILES - 1) or u == 1:
                 quantize_weights(t + 1)
-            if u + 1 < len(units):
-                ahead = first_stage(*units[u + 1])
-            if u > 0:
-                put(t, add_and_turn(*current)[:], wgs_half, idx2, h)
-            if h == 1:
-                if t > 0:
-                    prepare_early(t - 1)
+            if 0 < u < len(units) - 1:
+                products[u + 1] = first_stage(*units[u + 1])
+            if t > 0:
+                put(t, add_and_turn(*products[u])[:], wgs_half, idx2, h)
+            if h == 1 and t > 0:
+                prepare_early(t - 1)
+            if h == 1 and t < TILES - 1:
                 fetched[t] = keep.tile([P, HALF], F32, name="fetched", bufs=2)
                 fetch(t, 0, fetched[t][:])
-        prepare_early(TILES - 1)
+
+        t = TILES - 1
+        xs[t, 0] = keep.tile([P, HALF], F32, name="x%d" % t)
+        for q in range(2):
+            piece = keep.tile([P, HALF // 2], F32, name="piece", bufs=2)
+            fetch(t, q * HALF // 2, piece[:])
+            prepare(t, piece[:], xs[t, 0][:, q * HALF // 2 : (q + 1) * HALF // 2], turned0[:, 2 * q : 2 * q + 2, :])
 
         w4_codes = keep.tile([P, H], U32, name="w4_codes", align_bytes=64)
         nc.sync.dma_start(w4_codes[:].bitcast(I32), w4_words[0].rearrange("p n i -> p (n i)").bitcast(I32))
+        load_scale_rows(w4_plane, w4_scales)
         wgo_half = [load_half(wgo, h, "wgo%d" % h) for h in range(HALVES)]
 
         late = keep.tile([P, TILES - 1, HALF], F32, name="late", tag="wgs1")
         for t in range(TILES - 1):
-            fetch(t, 1, late[:, t, :])
+            fetch(t, HALF, late[:, t, :])
         grouped0 = keep.tile([P, HALF * PACK], BF16, name="grouped0", tag="grouped0", align_bytes=64)
-        x_codes = [quantize_half(turned0, grouped0, "x0")]
+        x_codes = [quantize_half([turned0[:, 0:2, :], turned0[:, 2:4, :]], grouped0, "x0")]
         last = keep.tile([P, HALF], F32, name="last", tag="grouped0", align_bytes=64)
-        fetch(TILES - 1, 1, last[:])
+        fetch(TILES - 1, HALF, last[:])
 
-        def second_stage(t, h, result):
+        def mix(t, h):
             bank = psum.tile([P, HALF], F32, name="mixed", tag="second", bufs=2)
             cols = slice(P * t, P * (t + 1))
             nc.tensor.matmul_mx(
                 bank[:], lhsT=w4_codes[:, cols].bitcast(FP8X4), lhsT_scale=w4_plane[:, 0, cols],
                 rhs=x_codes[h][0][:].bitcast(FP8X4), rhs_scale=x_codes[h][1][:], start=True, stop=True,
             )
-            nc.vector.scalar_tensor_tensor(result, sizes[t, h], gains[:, t : t + 1], bank[:], ALU.mult, ALU.add)
+            return bank
 
-        sizes1 = keep.tile([P, TILES, HALF], F32, name="sizes1", tag="turned0")
-        turned1 = keep.tile([P, BLOCKS, H], BF16, name="turned1")
-        results = {}
-        for t in range(TILES - 1):
-            results[t] = keep.tile([P, HALF], F32, name="result", bufs=3)
-            second_stage(t, 0, results[t][:])
-            if t > 0:
-                put(t - 1, results[t - 1][:], wgo_half, idx4, 0)
+        def second_stage(t, h, result):
+            nc.vector.tensor_tensor(result, mix(t, h)[:], xs[t, h][:], ALU.add)
+
+        def second_stage_turned(t, h, result):
+            blocks = [slice(P * b, P * (b + 1)) for b in range(BLOCKS)]
+            mixed = keep.tile([P, HALF], F32, name="mixed_sb", tag="turned1")
+            nc.scalar.copy(mixed[:], mix(t, h)[:])
+            summed = psum.tile([P, HALF], F32, name="first")
+            for cols in blocks:
+                nc.tensor.matmul(summed[:, cols], xs[t, h][:, cols], ident[:], start=True, stop=False, is_transpose=True)
+                nc.tensor.matmul(summed[:, cols], mixed[:, cols], ident[:], start=False, stop=True, is_transpose=True)
+            summed_sb = keep.tile([P, HALF], F32, name="summed_sb", bufs=2)
+            nc.scalar.copy(summed_sb[:], summed[:])
+            back = psum.tile([P, HALF], F32, name="third")
+            for cols in blocks:
+                nc.tensor.transpose(back[:, cols], summed_sb[:, cols], ident[:])
+            nc.scalar.copy(result, back[:])
+
+        late_size = keep.tile([P, TILES, HALF], F32, name="late_size", tag="turned0")
+        late_x = keep.tile([P, TILES, HALF], F32, name="late_x")
+        turned1 = keep.tile([P, BLOCKS, H], BF16, name="turned1", tag="turned1")
+        for t in range(2):
+            result = keep.tile([P, HALF], F32, name="result", bufs=3)
+            second_stage(t, 0, result[:])
+            put(t, result[:], wgo_half, idx4, 0)
         for t in range(TILES):
-            sizes[t, 1] = sizes1[:, t, :]
-            prepare(t, late[:, t, :] if t < TILES - 1 else last[:], sizes[t, 1], turned1)
+            xs[t, 1] = late_x[:, t, :]
+            prepare(t, late[:, t, :] if t < TILES - 1 else last[:], xs[t, 1], turned1[:], late_size[:, t, :])
         grouped1 = keep.tile([P, HALF * PACK], BF16, name="grouped1", tag="grouped1", align_bytes=64)
-        x_codes.append(quantize_half(turned1, grouped1, "x1"))
-        put(TILES - 2, results[TILES - 2][:], wgo_half, idx4, 0)
-        held = keep.tile([P, HALF], F32, name="held", tag="grouped1", align_bytes=64)
-        second_stage(TILES - 1, 0, held[:])
-        previous = (TILES - 1, held, 0)
+        x_codes.append(quantize_half([turned1[:, 0:2, :], turned1[:, 2:4, :]], grouped1, "x1"))
+        held = keep.tile([P, 2, HALF], F32, name="held", tag="grouped1", align_bytes=64)
+        second_stage(2, 0, held[:, 0, :])
+        put(2, held[:, 0, :], wgo_half, idx4, 0)
+        second_stage_turned(3, 0, held[:, 1, :])
+        put(3, held[:, 1, :], wgo_half, idx4, 0)
         for t in range(TILES):
             result = keep.tile([P, HALF], F32, name="result", bufs=3)
-            second_stage(t, 1, result[:])
-            put(previous[0], previous[1][:], wgo_half, idx4, previous[2])
-            if previous[2] == 1:
-                nc.sync.dma_start(out[P * previous[0] : P * (previous[0] + 1), :], pages[previous[0]][:])
-            previous = (t, result, 1)
-        put(previous[0], previous[1][:], wgo_half, idx4, 1)
-        nc.sync.dma_start(out[P * previous[0] : P * (previous[0] + 1), :], pages[previous[0]][:])
+            second_stage_turned(t, 1, result[:])
+            put(t, result[:], wgo_half, idx4, 1)
+            nc.sync.dma_start(out[P * t : P * (t + 1), :], pages[t][:])

@@ -52,11 +52,11 @@ def tile_list_short_shot_slots_kernel(
                     source[:, 4 * q : 4 * q + 4, :].rearrange("a r n -> r a n").bitcast(I32),
                 )
 
-        def load_weight(source, t):
-            raw = keep.tile([P, PACK, PASSES, P], F32, name="w_raw", bufs=4)
-            for a in range(PASSES):
+        def load_weight(source, t, passes, name="w_raw", bufs=4):
+            raw = keep.tile([P, PACK, len(passes), P], F32, name=name, bufs=bufs)
+            for i, a in enumerate(passes):
                 rows = source[512 * a : 512 * (a + 1), P * t : P * (t + 1)]
-                nc.sync.dma_start(raw[:, :, a, :], rows.rearrange("(p j) c -> p j c", j=PACK))
+                nc.sync.dma_start(raw[:, :, i, :], rows.rearrange("(p j) c -> p j c", j=PACK))
             return raw
 
         def load_w2(first, count):
@@ -81,7 +81,8 @@ def tile_list_short_shot_slots_kernel(
             return tile
 
         table_scales = keep.tile([P, PASSES, T], U8, name="table_scales")
-        nc.vector.memset(table_scales[:].bitcast(I32), 0)
+        nc.gpsimd.memset(table_scales[:, 0, :].bitcast(I32), 0)
+        nc.vector.memset(table_scales[:, 1, :].bitcast(I32), 0)
 
         w2_planes = keep.tile([P, PASSES, H], U8, name="w2_planes", align_bytes=64)
         w4_plane = keep.tile([P, 1, H], U8, name="w4_plane", align_bytes=64)
@@ -89,6 +90,8 @@ def tile_list_short_shot_slots_kernel(
         ident = keep.tile([P, P], F32, name="ident")
         make_identity(nc, ident[:])
         nc.gpsimd.memset(w4_plane[:].bitcast(I32), 0)
+        gain_rows = keep.tile([P, P], F32, name="gain_rows")
+        nc.gpsimd.memset(gain_rows[:], 0.0)
 
         raw1, raw3, pages = {}, {}, {}
         idx = load_list(offs, "idx")
@@ -96,34 +99,35 @@ def tile_list_short_shot_slots_kernel(
         idx3 = load_list(offs3, "idx3")
         idx4 = load_list(offs4, "idx4")
         w2_codes = load_w2(0, 1)
-        raw1[0] = load_weight(w1, 0)
-        raw3[0] = load_weight(w3, 0)
+        raw1[0] = load_weight(w1, 0, range(PASSES))
+        opening3 = [load_weight(w3, 0, [0], "w3_first", 1)]
         load_scale_rows(table_scales, tab_scales)
-        table = [load_table(0), load_table(1)]
+        nc.sync.dma_start(gain_rows[0:TILES, :], gain.rearrange("(t p) -> t p", p=P))
+        table = [load_table(0)]
         load_scale_rows(w2_planes, w2_scales)
+        table.append(load_table(1))
+        opening3.append(load_weight(w3, 0, [1], "w3_second", 1))
         pages[0] = load_page(0)
         wgs_half = [load_half(wgs, 0, "wgs0")]
-        raw1[1] = load_weight(w1, 1)
+        raw1[1] = load_weight(w1, 1, range(PASSES))
         w2_codes.extend(load_w2(1, TILES - 1))
-        raw3[1] = load_weight(w3, 1)
-        gains = keep.tile([P, TILES], F32, name="gains")
-        with nc.allow_non_contiguous_dma(reason="one gain for each row of a page tile"):
-            nc.sync.dma_start(gains[:], gain.rearrange("(t p) -> p t", p=P))
+        raw3[1] = load_weight(w3, 1, range(PASSES))
+        raw1[2] = load_weight(w1, 2, range(PASSES))
         wgs_half.append(load_half(wgs, 1, "wgs1"))
 
         codes1, codes3 = {}, {}
 
         def quantize_weight(raw, name):
-            grouped = keep.tile([P, PASSES, P, PACK], BF16, name="w_grouped", bufs=3, align_bytes=64)
-            nc.scalar.activation(
+            passes = raw.shape[2]
+            grouped = keep.tile([P, passes, P, PACK], BF16, name="w_grouped", bufs=3, align_bytes=64)
+            nc.scalar.copy(
                 grouped[:].rearrange("p a (c i) j -> p (a c) j i", i=4),
                 raw[:].rearrange("p j a (c i) -> p (a c) j i", i=4),
-                ACT.Copy,
             )
-            codes = keep.tile([P, PASSES * P], U32, name=name + "_codes", align_bytes=64)
-            plane = keep.tile([P, PASSES * P], U8, name=name + "_plane", align_bytes=64)
+            codes = keep.tile([P, passes * P], U32, name=name + "_codes", align_bytes=64)
+            plane = keep.tile([P, passes * P], U8, name=name + "_plane", align_bytes=64)
             nc.vector.quantize_mx(codes[:].bitcast(FP8X4), plane[:], grouped[:].rearrange("p a c j -> p (a c j)"))
-            return codes, plane
+            return [(codes[:, P * a : P * (a + 1)].bitcast(FP8X4), plane[:, P * a : P * (a + 1)]) for a in range(passes)]
 
         def quantize_weights(t):
             codes1[t] = quantize_weight(raw1[t], "w1_%d" % t)
@@ -136,7 +140,8 @@ def tile_list_short_shot_slots_kernel(
                 nc.vector.tensor_copy(plane[:], table_scales[:, a, :].indirect(half_of(idx, h)))
                 picked_scales[a, h] = plane
             if h == 0:
-                quantize_weights(0)
+                codes1[0] = quantize_weight(raw1[0], "w1_0")
+                codes3[0] = quantize_weight(opening3[0], "w3_00") + quantize_weight(opening3[1], "w3_01")
             for a in range(PASSES):
                 words = keep.tile([P, HALF], U32, name="picked_words%d%d" % (a, h), align_bytes=64)
                 nc.vector.tensor_copy(words[:], table[a][:].indirect(half_of(idx, h)))
@@ -144,28 +149,19 @@ def tile_list_short_shot_slots_kernel(
 
         def weight_operands(t):
             cols = slice(P * t, P * (t + 1))
-            by_pass = [slice(P * a, P * (a + 1)) for a in range(PASSES)]
-            return (
-                [(codes1[t][0][:, c].bitcast(FP8X4), codes1[t][1][:, c]) for c in by_pass],
-                [(w2_codes[t][:, a, :].bitcast(FP4X4), w2_planes[:, a, cols]) for a in range(PASSES)],
-                [(codes3[t][0][:, c].bitcast(FP8X4), codes3[t][1][:, c]) for c in by_pass],
-            )
+            second = [(w2_codes[t][:, a, :].bitcast(FP4X4), w2_planes[:, a, cols]) for a in range(PASSES)]
+            return codes1[t], second, codes3[t]
 
-        def product_banks():
+        def smaller_of(first, second, low):
+            first_sb = keep.tile([P, HALF], F32, name="first_sb", bufs=2)
+            nc.scalar.copy(first_sb[:], first[:])
+            nc.vector.tensor_tensor(low[:], second[:], first_sb[:], ALU.min)
+
+        def opening_stage(h):
             first = psum.tile([P, HALF], F32, name="first")
             second = psum.tile([P, HALF], F32, name="second", bufs=2)
             third = psum.tile([P, HALF], F32, name="third")
-            return first, second, third
-
-        def smaller_of(first, second):
-            first_sb = keep.tile([P, HALF], F32, name="first_sb", bufs=2)
-            nc.scalar.copy(first_sb[:], first[:])
-            low = keep.tile([P, HALF], F32, name="low", bufs=2)
-            nc.vector.tensor_tensor(low[:], second[:], first_sb[:], ALU.min)
-            return low
-
-        def opening_stage(h):
-            banks = product_banks()
+            banks = (first, second, third)
             for bank, operands in zip(banks, weight_operands(0)):
                 for a, (codes, plane) in enumerate(operands):
                     nc.tensor.matmul_mx(
@@ -173,31 +169,42 @@ def tile_list_short_shot_slots_kernel(
                         rhs=picked_words[a, h][:].bitcast(FP8X4), rhs_scale=picked_scales[a, h][:],
                         start=(a == 0), stop=(a == PASSES - 1),
                     )
-            low = smaller_of(banks[0], banks[1])
+            low = keep.tile([P, HALF], F32, name="opening_low")
+            smaller_of(first, second, low)
             hidden = keep.tile([P, HALF], F32, name="hidden", bufs=3)
             nc.vector.tensor_tensor(hidden[:], banks[2][:], low[:], ALU.add)
             return hidden
 
-        def first_stage(t, h):
-            banks = product_banks()
-            for bank, operands in zip(banks, weight_operands(t)):
-                for a, (codes, plane) in enumerate(operands):
-                    for b in range(BLOCKS):
-                        entries = slice(P * b, P * (b + 1))
-                        nc.tensor.matmul_mx(
-                            bank[:, entries],
-                            lhsT=picked_words[a, h][:, entries].bitcast(FP8X4),
-                            lhsT_scale=picked_scales[a, h][:, entries],
-                            rhs=codes,
-                            rhs_scale=plane,
-                            start=(a == 0 and b == 0),
-                            stop=(a == PASSES - 1 and b == BLOCKS - 1),
-                        )
-            low = smaller_of(banks[0], banks[1])
-            tag = "sizes%d" % (t - 1) if h == 1 and t > 0 else "third_sb%d" % h
+        def turned_product(bank, operands, h):
+            for a, (codes, plane) in enumerate(operands):
+                for b in range(BLOCKS):
+                    entries = slice(P * b, P * (b + 1))
+                    nc.tensor.matmul_mx(
+                        bank[:, entries],
+                        lhsT=picked_words[a, h][:, entries].bitcast(FP8X4),
+                        lhsT_scale=picked_scales[a, h][:, entries],
+                        rhs=codes,
+                        rhs_scale=plane,
+                        start=(a == 0 and b == 0),
+                        stop=(a == PASSES - 1 and b == BLOCKS - 1),
+                    )
+
+        def turned_minimum(t, h):
+            first = psum.tile([P, HALF], F32, name="first")
+            second = psum.tile([P, HALF], F32, name="second", bufs=2)
+            turned_product(first, weight_operands(t)[0], h)
+            turned_product(second, weight_operands(t)[1], h)
+            low = keep.tile([P, HALF], F32, name="low", bufs=2)
+            smaller_of(first, second, low)
+            return low
+
+        def turned_third(t, h):
+            third = psum.tile([P, HALF], F32, name="third")
+            turned_product(third, weight_operands(t)[2], h)
+            tag = "sizes%d" % (t - 1) if h == 1 else "third_sb"
             third_sb = keep.tile([P, HALF], F32, name="third_sb", tag=tag)
-            nc.scalar.copy(third_sb[:], banks[2][:])
-            return low, third_sb
+            nc.scalar.copy(third_sb[:], third[:])
+            return third_sb
 
         def add_and_turn(low, third_sb):
             summed = psum.tile([P, HALF], F32, name="summed")
@@ -245,6 +252,11 @@ def tile_list_short_shot_slots_kernel(
             nc.vector.quantize_mx(codes[:].bitcast(FP8X4), plane[:], grouped[:])
             return codes, plane
 
+        gain_bank = psum.tile([P, P], F32, name="gain_bank", tag="pairs", bufs=3)
+        nc.tensor.transpose(gain_bank[:], gain_rows[:], ident[:])
+        gains = keep.tile([P, TILES], F32, name="gains")
+        nc.scalar.activation(gains[:], gain_bank[:, 0:TILES], ACT.Copy)
+
         xs = {}
         turned0 = keep.tile([P, BLOCKS, H], BF16, name="turned0", tag="turned0")
         units = [(t, h) for t in range(TILES) for h in range(HALVES)]
@@ -255,11 +267,12 @@ def tile_list_short_shot_slots_kernel(
             xs[t, 0] = keep.tile([P, HALF], F32, name="x%d" % t)
             prepare(t, fetched[t][:], xs[t, 0][:], turned0[:], size[:])
 
-        products = {}
+        lows, thirds = {}, {}
         for u, (t, h) in enumerate(units):
             if h == 0 and t + 2 < TILES:
-                raw1[t + 2] = load_weight(w1, t + 2)
-                raw3[t + 2] = load_weight(w3, t + 2)
+                if t > 0:
+                    raw1[t + 2] = load_weight(w1, t + 2, range(PASSES))
+                raw3[t + 2] = load_weight(w3, t + 2, range(PASSES))
             if h == 0 and t + 1 < TILES:
                 pages[t + 1] = load_page(t + 1)
             if t == 0:
@@ -267,9 +280,11 @@ def tile_list_short_shot_slots_kernel(
             if (h == 0 and 0 < t < TILES - 1) or u == 1:
                 quantize_weights(t + 1)
             if 0 < u < len(units) - 1:
-                products[u + 1] = first_stage(*units[u + 1])
+                lows[u + 1] = turned_minimum(*units[u + 1])
             if t > 0:
-                put(t, add_and_turn(*products[u])[:], wgs_half, idx2, h)
+                put(t, add_and_turn(lows[u], thirds[u])[:], wgs_half, idx2, h)
+            if 0 < u < len(units) - 1:
+                thirds[u + 1] = turned_third(*units[u + 1])
             if h == 1 and t > 0:
                 prepare_early(t - 1)
             if h == 1 and t < TILES - 1:

from contextlib import ExitStack

import concourse.mybir as mybir
from concourse.masks import make_identity

K, H, T, S, T2 = 1024, 512, 4096, 1024, 2048
FLOPS = 2 * (3 * K * H * S + H * H * S)

F32 = mybir.dt.float32
BF16 = mybir.dt.bfloat16
I32 = mybir.dt.int32
U32 = mybir.dt.uint32
U16 = mybir.dt.uint16
U8 = mybir.dt.uint8
FP8X4 = mybir.dt.float8_e4m3fn_x4
FP4X4 = mybir.dt.float4_e2m1fn_x4
ALU = mybir.AluOpType
ACT = mybir.ActivationFunctionType

P = 128
PACK = 4
PASSES = K // (P * PACK)
TILES = H // P
HALF = 512
HALVES = S // HALF
BLOCKS = HALF // P
LIST_COLS = HALF // 16


def tile_list_short_shot_slots_kernel(
    tc, tab_words, tab_scales, offs, w1, w2_words, w2_scales, w3, page0, wgs, offs2, offs3, gain,
    w4_words, w4_scales, wgo, offs4, out,
):
    nc = tc.nc
    with ExitStack() as ctx:
        lists = ctx.enter_context(tc.tile_pool(name="lists", bufs=1))
        keep = ctx.enter_context(tc.tile_pool(name="keep", bufs=1))
        psum = ctx.enter_context(tc.psum_pool(name="psum", bufs=1))

        def half_of(list_tile, h):
            return list_tile[:, h * LIST_COLS : (h + 1) * LIST_COLS]

        def load_list(source, name):
            tile = lists.tile([P, S // 16], U16, name=name)
            nc.sync.dma_start(tile[:], source)
            return tile

        def load_scale_rows(tile, source):
            for q in range(4):
                nc.sync.dma_start(
                    tile[32 * q : 32 * q + 4].bitcast(I32),
                    source[:, 4 * q : 4 * q + 4, :].rearrange("a r n -> r a n").bitcast(I32),
                )

        def load_weight(source, t, passes, name="w_raw", bufs=4):
            raw = keep.tile([P, PACK, len(passes), P], F32, name=name, bufs=bufs)
            for i, a in enumerate(passes):
                rows = source[512 * a : 512 * (a + 1), P * t : P * (t + 1)]
                nc.sync.dma_start(raw[:, :, i, :], rows.rearrange("(p j) c -> p j c", j=PACK))
            return raw

        def load_w2(first, count):
            tile = keep.tile([P, PASSES, 2 * P * count], U8, name="w2_codes%d" % first, align_bytes=64)
            words = w2_words[:, :, 2 * P * first : 2 * P * (first + count)]
            nc.sync.dma_start(tile[:].bitcast(I32), words.rearrange("a p n -> p a n").bitcast(I32))
            return [tile[:, :, 2 * P * i : 2 * P * (i + 1)] for i in range(count)]

        def load_page(t):
            page = keep.tile([P, T2], F32, name="page%d" % t)
            nc.sync.dma_start(page[:], page0[P * t : P * (t + 1), :])
            return page

        def load_half(source, h, name):
            tile = keep.tile([P, HALF], F32, name=name)
            nc.sync.dma_start(tile[:], source[:, h * HALF : (h + 1) * HALF])
            return tile

        def load_table(a):
            tile = keep.tile([P, T], U32, name="table%d" % a)
            nc.sync.dma_start(tile[:].bitcast(I32), tab_words[a].rearrange("p n i -> p (n i)").bitcast(I32))
            return tile

        table_scales = keep.tile([P, PASSES, T], U8, name="table_scales")
        nc.gpsimd.memset(table_scales[:, 0, :].bitcast(I32), 0)
        nc.vector.memset(table_scales[:, 1, :].bitcast(I32), 0)

        w2_planes = keep.tile([P, PASSES, H], U8, name="w2_planes", align_bytes=64)
        w4_plane = keep.tile([P, 1, H], U8, name="w4_plane", align_bytes=64)
        nc.gpsimd.memset(w2_planes[:].bitcast(I32), 0)
        ident = keep.tile([P, P], F32, name="ident")
        make_identity(nc, ident[:])
        nc.gpsimd.memset(w4_plane[:].bitcast(I32), 0)
        gain_rows = keep.tile([P, P], F32, name="gain_rows")
        nc.gpsimd.memset(gain_rows[:], 0.0)

        raw1, raw3, pages = {}, {}, {}
        idx = load_list(offs, "idx")
        idx2 = load_list(offs2, "idx2")
        idx3 = load_list(offs3, "idx3")
        idx4 = load_list(offs4, "idx4")
        w2_codes = load_w2(0, 1)
        raw1[0] = load_weight(w1, 0, range(PASSES))
        opening3 = [load_weight(w3, 0, [0], "w3_first", 1)]
        load_scale_rows(table_scales, tab_scales)
        nc.sync.dma_start(gain_rows[0:TILES, :], gain.rearrange("(t p) -> t p", p=P))
        table = [load_table(0)]
        load_scale_rows(w2_planes, w2_scales)
        table.append(load_table(1))
        opening3.append(load_weight(w3, 0, [1], "w3_second", 1))
        pages[0] = load_page(0)
        wgs_half = [load_half(wgs, 0, "wgs0")]
        raw1[1] = load_weight(w1, 1, range(PASSES))
        w2_codes.extend(load_w2(1, TILES - 1))
        raw3[1] = load_weight(w3, 1, range(PASSES))
        raw1[2] = load_weight(w1, 2, range(PASSES))
        wgs_half.append(load_half(wgs, 1, "wgs1"))

        codes1, codes3 = {}, {}

        def quantize_weight(raw, name):
            passes = raw.shape[2]
            grouped = keep.tile([P, passes, P, PACK], BF16, name="w_grouped", bufs=3, align_bytes=64)
            nc.scalar.copy(
                grouped[:].rearrange("p a (c i) j -> p (a c) j i", i=4),
                raw[:].rearrange("p j a (c i) -> p (a c) j i", i=4),
            )
            codes = keep.tile([P, passes * P], U32, name=name + "_codes", align_bytes=64)
            plane = keep.tile([P, passes * P], U8, name=name + "_plane", align_bytes=64)
            nc.vector.quantize_mx(codes[:].bitcast(FP8X4), plane[:], grouped[:].rearrange("p a c j -> p (a c j)"))
            return [(codes[:, P * a : P * (a + 1)].bitcast(FP8X4), plane[:, P * a : P * (a + 1)]) for a in range(passes)]

        def quantize_weights(t):
            codes1[t] = quantize_weight(raw1[t], "w1_%d" % t)
            codes3[t] = quantize_weight(raw3[t], "w3_%d" % t)

        picked_words, picked_scales = {}, {}
        for h in range(HALVES):
            for a in range(PASSES):
                plane = keep.tile([P, HALF], U8, name="picked_scales%d%d" % (a, h), align_bytes=64)
                nc.vector.tensor_copy(plane[:], table_scales[:, a, :].indirect(half_of(idx, h)))
                picked_scales[a, h] = plane
            if h == 0:
                codes1[0] = quantize_weight(raw1[0], "w1_0")
                codes3[0] = quantize_weight(opening3[0], "w3_00") + quantize_weight(opening3[1], "w3_01")
            for a in range(PASSES):
                words = keep.tile([P, HALF], U32, name="picked_words%d%d" % (a, h), align_bytes=64)
                nc.vector.tensor_copy(words[:], table[a][:].indirect(half_of(idx, h)))
                picked_words[a, h] = words

        def weight_operands(t):
            cols = slice(P * t, P * (t + 1))
            second = [(w2_codes[t][:, a, :].bitcast(FP4X4), w2_planes[:, a, cols]) for a in range(PASSES)]
            return codes1[t], second, codes3[t]

        def smaller_of(first, second, low):
            first_sb = keep.tile([P, HALF], F32, name="first_sb", bufs=2)
            nc.scalar.copy(first_sb[:], first[:])
            nc.vector.tensor_tensor(low[:], second[:], first_sb[:], ALU.min)

        def opening_stage(h):
            first = psum.tile([P, HALF], F32, name="first")
            second = psum.tile([P, HALF], F32, name="second", bufs=2)
            third = psum.tile([P, HALF], F32, name="third")
            banks = (first, second, third)
            for bank, operands in zip(banks, weight_operands(0)):
                for a, (codes, plane) in enumerate(operands):
                    nc.tensor.matmul_mx(
                        bank[:], lhsT=codes, lhsT_scale=plane,
                        rhs=picked_words[a, h][:].bitcast(FP8X4), rhs_scale=picked_scales[a, h][:],
                        start=(a == 0), stop=(a == PASSES - 1),
                    )
            low = keep.tile([P, HALF], F32, name="opening_low")
            smaller_of(first, second, low)
            hidden = keep.tile([P, HALF], F32, name="hidden", bufs=3)
            nc.vector.tensor_tensor(hidden[:], banks[2][:], low[:], ALU.add)
            return hidden

        def turned_product(bank, operands, h):
            for a, (codes, plane) in enumerate(operands):
                for b in range(BLOCKS):
                    entries = slice(P * b, P * (b + 1))
                    nc.tensor.matmul_mx(
                        bank[:, entries],
                        lhsT=picked_words[a, h][:, entries].bitcast(FP8X4),
                        lhsT_scale=picked_scales[a, h][:, entries],
                        rhs=codes,
                        rhs_scale=plane,
                        start=(a == 0 and b == 0),
                        stop=(a == PASSES - 1 and b == BLOCKS - 1),
                    )

        def turned_minimum(t, h):
            first = psum.tile([P, HALF], F32, name="first")
            second = psum.tile([P, HALF], F32, name="second", bufs=2)
            turned_product(first, weight_operands(t)[0], h)
            turned_product(second, weight_operands(t)[1], h)
            low = keep.tile([P, HALF], F32, name="low", bufs=2)
            smaller_of(first, second, low)
            return low

        def turned_third(t, h):
            third = psum.tile([P, HALF], F32, name="third")
            turned_product(third, weight_operands(t)[2], h)
            tag = "sizes%d" % (t - 1) if h == 1 else "third_sb"
            third_sb = keep.tile([P, HALF], F32, name="third_sb", tag=tag)
            nc.scalar.copy(third_sb[:], third[:])
            return third_sb

        def add_and_turn(low, third_sb):
            summed = psum.tile([P, HALF], F32, name="summed")
            for b in range(BLOCKS):
                cols = slice(P * b, P * (b + 1))
                nc.tensor.matmul(summed[:, cols], third_sb[:, cols], ident[:], start=True, stop=False, is_transpose=True)
                nc.tensor.matmul(summed[:, cols], low[:, cols], ident[:], start=False, stop=True, is_transpose=True)
            hidden = keep.tile([P, HALF], F32, name="hidden", bufs=3)
            nc.scalar.copy(hidden[:], summed[:])
            return hidden

        def put(t, values, weights, list_tile, h):
            nc.vector.tensor_tensor(pages[t][:].indirect(half_of(list_tile, h)), values, weights[h][:], ALU.mult)

        def fetch(t, first, dest):
            count = dest.shape[1]
            entries = idx3[:, first // 16 : (first + count) // 16]
            nc.vector.tensor_copy(dest, pages[t][:].indirect(entries))

        def prepare(t, fetched, x, turned, size=None):
            count = fetched.shape[1]
            if size is None:
                size = keep.tile([P, count], F32, name="size", bufs=2)[:]
            nc.scalar.activation(size, fetched, ACT.Abs)
            nc.scalar.activation(x, size, ACT.Copy, scale=gains[:, t : t + 1])
            bank = psum.tile([P, count // P, P], F32, name="turn", tag="pairs", bufs=3)
            for b in range(count // P):
                nc.tensor.transpose(bank[:, b, :], x[:, P * b : P * (b + 1)], ident[:])
            nc.scalar.copy(
                turned.rearrange("p b (u t q e) -> p t b u q e", u=2, t=TILES, e=2)[:, t],
                bank[:].rearrange("p b (q u e) -> p b u q e", u=2, e=2),
            )

        def quantize_half(turned, grouped, name):
            for i, quarter in enumerate(turned):
                pairs = quarter[:].bitcast(F32)
                bank = psum.tile([P, 2, 2, P], F32, name="pairs", bufs=3)
                for b in range(2):
                    for u in range(2):
                        nc.tensor.transpose(bank[:, b, u, :], pairs[:, b, P * u : P * (u + 1)], ident[:])
                dest = grouped[:, 2 * P * PACK * i : 2 * P * PACK * (i + 1)].bitcast(F32)
                nc.scalar.copy(dest.rearrange("p (b e u) -> p b e u", b=2, u=2), bank[:].rearrange("p b u e -> p b e u"))
            codes = keep.tile([P, HALF], U32, name=name + "_codes", align_bytes=64)
            plane = keep.tile([P, HALF], U8, name=name + "_plane", align_bytes=64)
            nc.vector.quantize_mx(codes[:].bitcast(FP8X4), plane[:], grouped[:])
            return codes, plane

        gain_bank = psum.tile([P, P], F32, name="gain_bank", tag="pairs", bufs=3)
        nc.tensor.transpose(gain_bank[:], gain_rows[:], ident[:])
        gains = keep.tile([P, TILES], F32, name="gains")
        nc.scalar.activation(gains[:], gain_bank[:, 0:TILES], ACT.Copy)

        xs = {}
        turned0 = keep.tile([P, BLOCKS, H], BF16, name="turned0", tag="turned0")
        units = [(t, h) for t in range(TILES) for h in range(HALVES)]
        fetched = {}

        def prepare_early(t):
            size = keep.tile([P, HALF], F32, name="size", tag="sizes%d" % t)
            xs[t, 0] = keep.tile([P, HALF], F32, name="x%d" % t)
            prepare(t, fetched[t][:], xs[t, 0][:], turned0[:], size[:])

        lows, thirds = {}, {}
        for u, (t, h) in enumerate(units):
            if h == 0 and t + 2 < TILES:
                if t > 0:
                    raw1[t + 2] = load_weight(w1, t + 2, range(PASSES))
                raw3[t + 2] = load_weight(w3, t + 2, range(PASSES))
            if h == 0 and t + 1 < TILES:
                pages[t + 1] = load_page(t + 1)
            if t == 0:
                put(t, opening_stage(h)[:], wgs_half, idx2, h)
            if (h == 0 and 0 < t < TILES - 1) or u == 1:
                quantize_weights(t + 1)
            if 0 < u < len(units) - 1:
                lows[u + 1] = turned_minimum(*units[u + 1])
            if t > 0:
                put(t, add_and_turn(lows[u], thirds[u])[:], wgs_half, idx2, h)
            if 0 < u < len(units) - 1:
                thirds[u + 1] = turned_third(*units[u + 1])
            if h == 1 and t > 0:
                prepare_early(t - 1)
            if h == 1 and t < TILES - 1:
                fetched[t] = keep.tile([P, HALF], F32, name="fetched", bufs=2)
                fetch(t, 0, fetched[t][:])

        t = TILES - 1
        xs[t, 0] = keep.tile([P, HALF], F32, name="x%d" % t)
        for q in range(2):
            piece = keep.tile([P, HALF // 2], F32, name="piece", bufs=2)
            fetch(t, q * HALF // 2, piece[:])
            prepare(t, piece[:], xs[t, 0][:, q * HALF // 2 : (q + 1) * HALF // 2], turned0[:, 2 * q : 2 * q + 2, :])

        w4_codes = keep.tile([P, H], U32, name="w4_codes", align_bytes=64)
        nc.sync.dma_start(w4_codes[:].bitcast(I32), w4_words[0].rearrange("p n i -> p (n i)").bitcast(I32))
        load_scale_rows(w4_plane, w4_scales)
        wgo_half = [load_half(wgo, h, "wgo%d" % h) for h in range(HALVES)]

        late = keep.tile([P, TILES - 1, HALF], F32, name="late", tag="wgs1")
        for t in range(TILES - 1):
            fetch(t, HALF, late[:, t, :])
        grouped0 = keep.tile([P, HALF * PACK], BF16, name="grouped0", tag="grouped0", align_bytes=64)
        x_codes = [quantize_half([turned0[:, 0:2, :], turned0[:, 2:4, :]], grouped0, "x0")]
        last = keep.tile([P, HALF], F32, name="last", tag="grouped0", align_bytes=64)
        fetch(TILES - 1, HALF, last[:])

        def mix(t, h):
            bank = psum.tile([P, HALF], F32, name="mixed", tag="second", bufs=2)
            cols = slice(P * t, P * (t + 1))
            nc.tensor.matmul_mx(
                bank[:], lhsT=w4_codes[:, cols].bitcast(FP8X4), lhsT_scale=w4_plane[:, 0, cols],
                rhs=x_codes[h][0][:].bitcast(FP8X4), rhs_scale=x_codes[h][1][:], start=True, stop=True,
            )
            return bank

        def second_stage(t, h, result):
            nc.vector.tensor_tensor(result, mix(t, h)[:], xs[t, h][:], ALU.add)

        def second_stage_turned(t, h, result):
            blocks = [slice(P * b, P * (b + 1)) for b in range(BLOCKS)]
            mixed = keep.tile([P, HALF], F32, name="mixed_sb", tag="turned1")
            nc.scalar.copy(mixed[:], mix(t, h)[:])
            summed = psum.tile([P, HALF], F32, name="first")
            for cols in blocks:
                nc.tensor.matmul(summed[:, cols], xs[t, h][:, cols], ident[:], start=True, stop=False, is_transpose=True)
                nc.tensor.matmul(summed[:, cols], mixed[:, cols], ident[:], start=False, stop=True, is_transpose=True)
            summed_sb = keep.tile([P, HALF], F32, name="summed_sb", bufs=2)
            nc.scalar.copy(summed_sb[:], summed[:])
            back = psum.tile([P, HALF], F32, name="third")
            for cols in blocks:
                nc.tensor.transpose(back[:, cols], summed_sb[:, cols], ident[:])
            nc.scalar.copy(result, back[:])

        late_size = keep.tile([P, TILES, HALF], F32, name="late_size", tag="turned0")
        late_x = keep.tile([P, TILES, HALF], F32, name="late_x")
        turned1 = keep.tile([P, BLOCKS, H], BF16, name="turned1", tag="turned1")
        for t in range(2):
            result = keep.tile([P, HALF], F32, name="result", bufs=3)
            second_stage(t, 0, result[:])
            put(t, result[:], wgo_half, idx4, 0)
        for t in range(TILES):
            xs[t, 1] = late_x[:, t, :]
            prepare(t, late[:, t, :] if t < TILES - 1 else last[:], xs[t, 1], turned1[:], late_size[:, t, :])
        grouped1 = keep.tile([P, HALF * PACK], BF16, name="grouped1", tag="grouped1", align_bytes=64)
        x_codes.append(quantize_half([turned1[:, 0:2, :], turned1[:, 2:4, :]], grouped1, "x1"))
        held = keep.tile([P, 2, HALF], F32, name="held", tag="grouped1", align_bytes=64)
        second_stage(2, 0, held[:, 0, :])
        put(2, held[:, 0, :], wgo_half, idx4, 0)
        second_stage_turned(3, 0, held[:, 1, :])
        put(3, held[:, 1, :], wgo_half, idx4, 0)
        for t in range(TILES):
            result = keep.tile([P, HALF], F32, name="result", bufs=3)
            second_stage_turned(t, 1, result[:])
            put(t, result[:], wgo_half, idx4, 1)
            nc.sync.dma_start(out[P * t : P * (t + 1), :], pages[t][:])
